import numpy as np
import ml_dtypes


def mxq(x, axis, fmt="e4m3"):
    dtype, down = {"e4m3": (ml_dtypes.float8_e4m3fn, 7), "e5m2": (ml_dtypes.float8_e5m2, 14)}[fmt]
    v = np.moveaxis(np.asarray(x, np.float32).astype(ml_dtypes.bfloat16).astype(np.float64), axis, -1)
    blocks = v.reshape(v.shape[:-1] + (-1, 32))
    amax = np.abs(blocks).max(-1, keepdims=True)
    byte = np.maximum(np.where(amax > 0, np.frexp(amax)[1] - 1 + 127, 0) - down, 1)
    scale = np.exp2(byte - 127.0)
    codes = (blocks / scale).astype(np.float32).astype(dtype).astype(np.float64)
    return np.moveaxis((codes * scale).reshape(v.shape), -1, axis)


WIDE = False


def mx_kscale(k):
    if not WIDE:
        return np.ones(k)
    levels = np.array([10, -10, 5, -5, 0])
    if k % 512:
        return np.exp2(np.random.permutation(np.resize(levels, k // 32))).repeat(32)
    a = np.empty((k // 512, 16))
    for p in range(k // 512):
        a[p, :8] = np.random.permutation(np.resize(levels, 8))
        for g in range(8):
            far = levels[np.abs(levels - a[p, g]) >= 10]
            a[p, g + 8] = far[np.random.randint(len(far))]
    return np.exp2(a.ravel()).repeat(32)


def f64(x):
    return np.asarray(x).astype(np.float64)


def striped(idx):
    return np.tile(idx.reshape(-1, 16).T, (8, 1)).astype(np.uint16)


def unstriped(offs):
    return offs[:16].T.reshape(-1).astype(np.int64)


def pack_weight(w):
    k, n = w.shape
    w = f64(np.asarray(w, np.float32).astype(ml_dtypes.bfloat16)).reshape(k // 32, 32, n)
    amax = np.abs(w).max(1)
    byte = np.clip(np.where(amax > 0, np.frexp(amax)[1] - 1 + 127 - 7, 1), 1, 254)
    scaled = (w * np.exp2(127.0 - byte)[:, None, :]).reshape(k, n).astype(np.float32)
    words = np.ascontiguousarray(scaled.reshape(k // 512, 128, 4, n).transpose(0, 1, 3, 2)).astype(ml_dtypes.float8_e4m3fn).view(np.uint8)
    return words, np.ascontiguousarray(byte.astype(np.uint8).reshape(k // 512, 16, n))


def unpack_weight(words, scales):
    g, p, n, _ = words.shape
    vals = np.ascontiguousarray(words).view(ml_dtypes.float8_e4m3fn).astype(np.float64) * np.repeat(np.exp2(scales.astype(np.float64) - 127.0), 8, axis=1)[..., None]
    return vals.transpose(0, 1, 3, 2).reshape(g * 512, n)


K, T, S, N, D = 512, 1024, 512, 128, 3
P = 2 ** 7


def setup_inputs():
    n = np.random.standard_normal
    s = mx_kscale(K)[:, None]
    packed_xT = pack_weight(n((K, T)) * s)
    return {
        "x_words": packed_xT[0],
        "x_scales": packed_xT[1],
        "w1": (n((K, N)) / np.sqrt(K) / s).astype(np.float32),
        "gain": (np.tile(np.random.uniform(0.05, 0.5, (D, 1, S)), (1, P, 1))).astype(np.float32),
        "owng": (np.tile(np.random.uniform(0.6, 1.6, S), (P, 1))).astype(np.float32),
        "goal": (np.random.uniform(0.4, 1.2, (N, 1))).astype(np.float32),
        "cap": (np.tile(np.random.uniform(0.5, 1.5, S), (P, 1))).astype(np.float32),
        "offs": striped(np.random.permutation(T)[:S]),
        "pos1": striped(np.random.permutation(S)[:S]),
        "pos2": striped(np.random.permutation(S)[:S]),
        "pos3": striped(np.random.permutation(S)[:S]),
    }


def reference(x_words, x_scales, w1, gain, owng, goal, cap, offs, pos1, pos2, pos3):
    xq = unpack_weight(x_words, x_scales)[:, unstriped(offs)]
    y = mxq(f64(w1), 0, "e4m3").T @ xq
    pw = np.exp(0.4 * y)
    ia = pw[:, unstriped(pos1)] * f64(gain)[0, :1] + pw[:, unstriped(pos2)] * f64(gain)[1, :1] + pw[:, unstriped(pos3)] * f64(gain)[2, :1] + 0.1
    pn = np.minimum(f64(goal) * (ia / f64(owng)[:1]), f64(cap)[:1])
    ib = pn[:, unstriped(pos1)] * f64(gain)[0, :1] + pn[:, unstriped(pos2)] * f64(gain)[1, :1] + pn[:, unstriped(pos3)] * f64(gain)[2, :1] + 0.1
    return np.minimum(f64(goal) * (ib / f64(owng)[:1]), f64(cap)[:1])

@@ -1,0 +1,167 @@
+from contextlib import ExitStack
+
+import concourse.mybir as mybir
+from concourse.masks import make_identity
+
+K, T, S, M, D = 512, 1024, 512, 128, 3
+P = 128
+PACK = 4
+HALF = S // 2
+FLOPS = 2 * K * M * S
+BYTES = K * T + 16 * T + 4 * K * M + 4 * (D + 2) * S + 4 * M + 4 * 2 * P * S // 16 + 4 * M * S
+
+F32 = mybir.dt.float32
+BF16 = mybir.dt.bfloat16
+I32 = mybir.dt.int32
+U32 = mybir.dt.uint32
+U16 = mybir.dt.uint16
+U8 = mybir.dt.uint8
+FP8X4 = mybir.dt.float8_e4m3fn_x4
+ALU = mybir.AluOpType
+ACT = mybir.ActivationFunctionType
+
+
+def tile_picked_yfosch_two_p_kernel(
+    tc, x_words, x_scales, w1, gain, owng, goal, cap, offs, pos1, pos2, pos3, out
+):
+    nc = tc.nc
+    with ExitStack() as ctx:
+        keep = ctx.enter_context(tc.tile_pool(name="keep", bufs=1))
+        psum = ctx.enter_context(tc.psum_pool(name="psum", bufs=1))
+
+        offs_sb = keep.tile([P, S // 16], U16, name="offs_sb")
+        pos_sb = [keep.tile([P, S // 16], U16, name="pos_sb%d" % d) for d in range(D)]
+        words = keep.tile([P, T], I32, name="words", align_bytes=64)
+        scales = keep.tile([P, T], U8, name="scales", align_bytes=64)
+        w_raw = keep.tile([P, PACK, M], F32, name="w_raw")
+        gain_c = keep.tile([P, 2, PACK], F32, name="gain_c")
+        owng_c = keep.tile([P, PACK], F32, name="owng_c")
+        goal_sb = keep.tile([P, 1], F32, name="goal_sb")
+        cap_sb = keep.tile([P, S], F32, name="cap_sb")
+
+        gain2_sb = keep.tile([P, S], F32, name="gain2_sb")
+        nc.sync.dma_start(offs_sb[:], offs)
+        for q, queue in enumerate((nc.sync, nc.scalar, nc.sync, nc.scalar)):
+            rows = x_scales[0, 4 * q : 4 * q + 4, :].bitcast(I32)
+            queue.dma_start(scales[32 * q : 32 * q + 32, :].bitcast(I32), rows.partition_broadcast(8))
+        nc.scalar.dma_start(owng_c[:], owng[0].rearrange("(p t) -> p t", t=PACK))
+        nc.sync.dma_start(words[:], x_words[0].rearrange("p n t -> p (n t)").bitcast(I32))
+        nc.sync.dma_start(w_raw[:], w1.rearrange("(p j) m -> p j m", j=PACK))
+        nc.sync.dma_start(gain_c[:], gain[0:2, 0, :].rearrange("d (p t) -> p d t", t=PACK))
+        nc.sync.dma_start(gain2_sb[:], gain[2])
+        for d, pos in ((2, pos3), (0, pos1), (1, pos2)):
+            nc.sync.dma_start(pos_sb[d][:], pos)
+        nc.sync.dma_start(goal_sb[:], goal)
+        nc.sync.dma_start(cap_sb[:], cap)
+
+        ident = keep.tile([P, P], F32, name="ident")
+        nc.vector.memset(ident[:], 0.0)
+        make_identity(nc, ident[:], nomemset=True)
+
+
+        w_bf = keep.tile([P, M, PACK], BF16, name="w_bf", align_bytes=64)
+        nc.scalar.activation(w_bf[:], w_raw[:].rearrange("p j m -> p m j"), ACT.Copy)
+
+        picked_scales = [keep.tile([P, HALF], U8, name="picked_scales%d" % h, align_bytes=64) for h in range(2)]
+        picked_words = [keep.tile([P, HALF], U32, name="picked_words%d" % h, align_bytes=64) for h in range(2)]
+
+        def offsets(lst, c0, c1):
+            return lst[:, c0 // 16 : c1 // 16]
+
+        for h in range(2):
+            nc.vector.tensor_copy(picked_scales[h][:], scales[:].indirect(offsets(offs_sb, h * HALF, (h + 1) * HALF)))
+        inv_c = keep.tile([P, PACK], F32, name="inv_c")
+        ratio_c = keep.tile([P, 2, PACK], F32, name="ratio_c")
+        nc.vector.reciprocal(inv_c[:], owng_c[:])
+        nc.vector.tensor_copy(picked_words[0][:], words[:].bitcast(U32).indirect(offsets(offs_sb, 0, HALF)))
+
+
+        w_codes = keep.tile([P, M], U32, name="w_codes", align_bytes=64)
+        w_scales = keep.tile([P, M], U8, name="w_scales", align_bytes=64)
+        nc.vector.quantize_mx(out=w_codes[:].bitcast(FP8X4), scales=w_scales[:], in_=w_bf[:].rearrange("p m j -> p (m j)"))
+        nc.vector.tensor_copy(picked_words[1][:], words[:].bitcast(U32).indirect(offsets(offs_sb, HALF, S)))
+        nc.vector.tensor_tensor(ratio_c[:], gain_c[:], inv_c[:].unsqueeze(1).to_broadcast([P, 2, PACK]), ALU.mult)
+
+        power = keep.tile([P, S], F32, name="power")
+        for h in range(2):
+            y = psum.tile([P, HALF], F32, name="y%d" % h)
+            nc.tensor.matmul_mx(
+                out=y[:],
+                lhsT=w_codes[:].bitcast(FP8X4),
+                lhsT_scale=w_scales[:],
+                rhs=picked_words[h][:].bitcast(FP8X4),
+                rhs_scale=picked_scales[h][:],
+                start=True,
+                stop=True,
+            )
+            nc.scalar.activation(power[:, h * HALF : (h + 1) * HALF], y[:], ACT.Exp, scale=0.4)
+
+        def spread(name, compact):
+            bank = psum.tile([P, PACK, P], F32, name=name)
+            for t in range(PACK):
+                nc.tensor.transpose(bank[:, t, :], compact[:, t : t + 1].to_broadcast([P, P]), ident[:])
+            return bank
+
+        ratio_ps = [None] * D
+        inv_ps = spread("inv", inv_c[:])
+        ratio_ps[0] = spread("ratio0", ratio_c[:, 0, :])
+        ratio_ps[1] = spread("ratio1", ratio_c[:, 1, :])
+
+        def link_order(bank, c0, c1):
+            return bank[:].rearrange("m t p -> m p t")[:, c0 // PACK : c1 // PACK, :]
+
+        def quads(ap):
+            return ap.rearrange("m (p t) -> m p t", t=PACK)
+
+
+        def one_round(r, window, result, store):
+            heard = [keep.tile([P, S], F32, name="heard%d_%d" % (r, d)) for d in range(D)]
+            term = [keep.tile([P, S], F32, name="term%d_%d" % (r, d)) for d in range(D)]
+            acc = [keep.tile([P, S], F32, name="acc%d_%d" % (r, d)) for d in range(D)]
+
+            def fetch(d, c0, c1):
+                nc.scalar.activation(heard[d][:, c0:c1], window[:].indirect(offsets(pos_sb[d], c0, c1)), ACT.Copy)
+
+            def weigh(d, c0, c1):
+                nc.vector.tensor_tensor(quads(term[d][:, c0:c1]), quads(heard[d][:, c0:c1]), link_order(ratio_ps[d], c0, c1), ALU.mult)
+
+            def noise(d, c0, c1):
+                nc.vector.scalar_tensor_tensor(quads(acc[0][:, c0:c1]), quads(term[d][:, c0:c1]), 0.1, link_order(inv_ps, c0, c1), ALU.add, ALU.mult)
+
+            def add(i, d, c0, c1):
+                nc.vector.tensor_tensor(acc[i][:, c0:c1], acc[i - 1][:, c0:c1], term[d][:, c0:c1], ALU.add)
+
+            def limit(c0, c1):
+                nc.vector.scalar_tensor_tensor(result[:, c0:c1], acc[2][:, c0:c1], goal_sb[:], cap_sb[:, c0:c1], ALU.mult, ALU.min)
+                if store:
+                    nc.sync.dma_start(out[:, c0:c1], result[:, c0:c1])
+
+            A = (0, HALF)
+            B = (HALF, S)
+            B0 = (HALF, HALF + HALF // 2)
+            B1 = (HALF + HALF // 2, S)
+            fetch(0, *A)
+            fetch(1, *A)
+            fetch(0, *B)
+            fetch(1, *B)
+            for c0, c1 in (A, B):
+                nc.vector.tensor_tensor(term[2][:, c0:c1], window[:].indirect(offsets(pos_sb[2], c0, c1)), gain2_sb[:, c0:c1], ALU.mult)
+            weigh(0, *A)
+            noise(2, *A)
+            weigh(1, *A)
+            noise(2, *B)
+            add(1, 0, *A)
+            weigh(0, *B)
+            add(2, 1, *A)
+            weigh(1, *B)
+            add(1, 0, *B)
+            limit(*A)
+            add(2, 1, *B0)
+            add(2, 1, *B1)
+            limit(*B0)
+            limit(*B1)
+
+        limited = keep.tile([P, S], F32, name="limited")
+        final = keep.tile([P, S], F32, name="final")
+        one_round(0, power, limited, False)
+        one_round(1, limited, final, True)

@@ -6,7 +6,7 @@ from concourse.masks import make_identity
 K, T, S, M, D = 512, 1024, 512, 128, 3
 P = 128
 PACK = 4
-HALF = S // 2
+BLOCKS = S // P
 FLOPS = 2 * K * M * S
 BYTES = K * T + 16 * T + 4 * K * M + 4 * (D + 2) * S + 4 * M + 4 * 2 * P * S // 16 + 4 * M * S
 
@@ -31,135 +31,128 @@ def tile_picked_yfosch_two_p_kernel(
 
         offs_sb = keep.tile([P, S // 16], U16, name="offs_sb")
         pos_sb = [keep.tile([P, S // 16], U16, name="pos_sb%d" % d) for d in range(D)]
-        words = keep.tile([P, T], I32, name="words", align_bytes=64)
+        words = keep.tile([P, T], I32, name="words", tag="table", align_bytes=64)
         scales = keep.tile([P, T], U8, name="scales", align_bytes=64)
         w_raw = keep.tile([P, PACK, M], F32, name="w_raw")
-        gain_c = keep.tile([P, 2, PACK], F32, name="gain_c")
-        owng_c = keep.tile([P, PACK], F32, name="owng_c")
+        gains = keep.tile([P, D, S], F32, name="gains")
+        owng_col = keep.tile([P, BLOCKS, 8], F32, name="owng_col")
         goal_sb = keep.tile([P, 1], F32, name="goal_sb")
         cap_sb = keep.tile([P, S], F32, name="cap_sb")
 
-        gain2_sb = keep.tile([P, S], F32, name="gain2_sb")
         nc.sync.dma_start(offs_sb[:], offs)
         for q, queue in enumerate((nc.sync, nc.scalar, nc.sync, nc.scalar)):
             rows = x_scales[0, 4 * q : 4 * q + 4, :].bitcast(I32)
             queue.dma_start(scales[32 * q : 32 * q + 32, :].bitcast(I32), rows.partition_broadcast(8))
-        nc.scalar.dma_start(owng_c[:], owng[0].rearrange("(p t) -> p t", t=PACK))
-        nc.sync.dma_start(words[:], x_words[0].rearrange("p n t -> p (n t)").bitcast(I32))
         nc.sync.dma_start(w_raw[:], w1.rearrange("(p j) m -> p j m", j=PACK))
-        nc.sync.dma_start(gain_c[:], gain[0:2, 0, :].rearrange("d (p t) -> p d t", t=PACK))
-        nc.sync.dma_start(gain2_sb[:], gain[2])
+        nc.sync.dma_start(words[:], x_words[0].rearrange("p n t -> p (n t)").bitcast(I32))
+        with nc.allow_non_contiguous_dma(reason="one value a partition and block"):
+            nc.sync.dma_start(owng_col[:, :, 0], owng[0].rearrange("(b p) -> p b", p=P))
         for d, pos in ((2, pos3), (0, pos1), (1, pos2)):
             nc.sync.dma_start(pos_sb[d][:], pos)
         nc.sync.dma_start(goal_sb[:], goal)
+        nc.sync.dma_start(gains[:], gain.rearrange("d p j -> p d j"))
         nc.sync.dma_start(cap_sb[:], cap)
 
         ident = keep.tile([P, P], F32, name="ident")
-        nc.vector.memset(ident[:], 0.0)
-        make_identity(nc, ident[:], nomemset=True)
+        make_identity(nc, ident[:])
 
-
-        w_bf = keep.tile([P, M, PACK], BF16, name="w_bf", align_bytes=64)
+        w_bf = keep.tile([P, M, PACK], BF16, name="w_bf", tag="stage", align_bytes=64)
         nc.scalar.activation(w_bf[:], w_raw[:].rearrange("p j m -> p m j"), ACT.Copy)
 
-        picked_scales = [keep.tile([P, HALF], U8, name="picked_scales%d" % h, align_bytes=64) for h in range(2)]
-        picked_words = [keep.tile([P, HALF], U32, name="picked_words%d" % h, align_bytes=64) for h in range(2)]
+        def offsets(lst, cols):
+            return lst[:, cols.start // 16 : cols.stop // 16]
 
-        def offsets(lst, c0, c1):
-            return lst[:, c0 // 16 : c1 // 16]
-
-        for h in range(2):
-            nc.vector.tensor_copy(picked_scales[h][:], scales[:].indirect(offsets(offs_sb, h * HALF, (h + 1) * HALF)))
-        inv_c = keep.tile([P, PACK], F32, name="inv_c")
-        ratio_c = keep.tile([P, 2, PACK], F32, name="ratio_c")
-        nc.vector.reciprocal(inv_c[:], owng_c[:])
-        nc.vector.tensor_copy(picked_words[0][:], words[:].bitcast(U32).indirect(offsets(offs_sb, 0, HALF)))
-
-
+        picked_scales = keep.tile([P, S], U8, name="picked_scales", align_bytes=64)
+        nc.vector.tensor_copy(picked_scales[:], scales[:].indirect(offs_sb[:]))
         w_codes = keep.tile([P, M], U32, name="w_codes", align_bytes=64)
         w_scales = keep.tile([P, M], U8, name="w_scales", align_bytes=64)
         nc.vector.quantize_mx(out=w_codes[:].bitcast(FP8X4), scales=w_scales[:], in_=w_bf[:].rearrange("p m j -> p (m j)"))
-        nc.vector.tensor_copy(picked_words[1][:], words[:].bitcast(U32).indirect(offsets(offs_sb, HALF, S)))
-        nc.vector.tensor_tensor(ratio_c[:], gain_c[:], inv_c[:].unsqueeze(1).to_broadcast([P, 2, PACK]), ALU.mult)
 
+        picked_words = keep.tile([P, S], U32, name="picked_words", tag="stage", align_bytes=64)
         power = keep.tile([P, S], F32, name="power")
-        for h in range(2):
-            y = psum.tile([P, HALF], F32, name="y%d" % h)
+        for i, cols in enumerate((slice(0, 256), slice(256, 384), slice(384, 512))):
+            nc.vector.tensor_copy(picked_words[:, cols], words[:].bitcast(U32).indirect(offsets(offs_sb, cols)))
+            y = psum.tile([P, cols.stop - cols.start], F32, name="y%d" % i)
             nc.tensor.matmul_mx(
                 out=y[:],
                 lhsT=w_codes[:].bitcast(FP8X4),
                 lhsT_scale=w_scales[:],
-                rhs=picked_words[h][:].bitcast(FP8X4),
-                rhs_scale=picked_scales[h][:],
+                rhs=picked_words[:, cols].bitcast(FP8X4),
+                rhs_scale=picked_scales[:, cols],
                 start=True,
                 stop=True,
             )
-            nc.scalar.activation(power[:, h * HALF : (h + 1) * HALF], y[:], ACT.Exp, scale=0.4)
+            nc.scalar.activation(power[:, cols], y[:], ACT.Exp, scale=0.4)
 
-        def spread(name, compact):
-            bank = psum.tile([P, PACK, P], F32, name=name)
-            for t in range(PACK):
-                nc.tensor.transpose(bank[:, t, :], compact[:, t : t + 1].to_broadcast([P, P]), ident[:])
-            return bank
+        inv_col = keep.tile([P, BLOCKS], F32, name="inv_col", tag="table", align_bytes=64)
+        noise_col = keep.tile([P, 2], F32, name="noise_col")
+        nc.vector.reciprocal(inv_col[:], owng_col[:, :, 0])
+        nc.vector.tensor_scalar(noise_col[:], inv_col[:, 0:2], 0.1, None, ALU.mult)
+        inv_row = psum.tile([P, 2 * P], F32, name="inv_row")
+        for b in range(2):
+            nc.tensor.transpose(inv_row[:, b * P : (b + 1) * P], inv_col[:, 2 + b : 3 + b].to_broadcast([P, P]), ident[:])
 
-        ratio_ps = [None] * D
-        inv_ps = spread("inv", inv_c[:])
-        ratio_ps[0] = spread("ratio0", ratio_c[:, 0, :])
-        ratio_ps[1] = spread("ratio1", ratio_c[:, 1, :])
-
-        def link_order(bank, c0, c1):
-            return bank[:].rearrange("m t p -> m p t")[:, c0 // PACK : c1 // PACK, :]
-
-        def quads(ap):
-            return ap.rearrange("m (p t) -> m p t", t=PACK)
-
+        block = [slice(b * P, (b + 1) * P) for b in range(BLOCKS)]
+        A = slice(0, 2 * P)
+        B = slice(2 * P, S)
 
         def one_round(r, window, result, store):
             heard = [keep.tile([P, S], F32, name="heard%d_%d" % (r, d)) for d in range(D)]
             term = [keep.tile([P, S], F32, name="term%d_%d" % (r, d)) for d in range(D)]
             acc = [keep.tile([P, S], F32, name="acc%d_%d" % (r, d)) for d in range(D)]
+            turned = [psum.tile([P, P], F32, name="turned%d" % b) for b in range(2)]
+            back = [psum.tile([P, P], F32, name="back%d" % b) for b in range(2)]
+            ratio_t = keep.tile([P, 2, P], F32, name="ratio_t%d" % r)
 
-            def fetch(d, c0, c1):
-                nc.scalar.activation(heard[d][:, c0:c1], window[:].indirect(offsets(pos_sb[d], c0, c1)), ACT.Copy)
+            def fetch(d, cols):
+                nc.scalar.activation(heard[d][:, cols], window[:].indirect(offsets(pos_sb[d], cols)), ACT.Copy)
 
-            def weigh(d, c0, c1):
-                nc.vector.tensor_tensor(quads(term[d][:, c0:c1]), quads(heard[d][:, c0:c1]), link_order(ratio_ps[d], c0, c1), ALU.mult)
+            def fused(d, cols):
+                nc.vector.tensor_tensor(term[d][:, cols], window[:].indirect(offsets(pos_sb[d], cols)), gains[:, d, cols], ALU.mult)
 
-            def noise(d, c0, c1):
-                nc.vector.scalar_tensor_tensor(quads(acc[0][:, c0:c1]), quads(term[d][:, c0:c1]), 0.1, link_order(inv_ps, c0, c1), ALU.add, ALU.mult)
+            def weigh(d, cols):
+                nc.vector.tensor_tensor(term[d][:, cols], heard[d][:, cols], gains[:, d, cols], ALU.mult)
 
-            def add(i, d, c0, c1):
-                nc.vector.tensor_tensor(acc[i][:, c0:c1], acc[i - 1][:, c0:c1], term[d][:, c0:c1], ALU.add)
+            def turn(d, first, last):
+                for b in range(2):
+                    nc.tensor.matmul(turned[b][:], term[d][:, block[b]], ident[:], start=first, stop=last, is_transpose=True)
 
-            def limit(c0, c1):
-                nc.vector.scalar_tensor_tensor(result[:, c0:c1], acc[2][:, c0:c1], goal_sb[:], cap_sb[:, c0:c1], ALU.mult, ALU.min)
+            def put(cols):
                 if store:
-                    nc.sync.dma_start(out[:, c0:c1], result[:, c0:c1])
+                    nc.sync.dma_start(out[:, cols], result[:, cols])
 
-            A = (0, HALF)
-            B = (HALF, S)
-            B0 = (HALF, HALF + HALF // 2)
-            B1 = (HALF + HALF // 2, S)
-            fetch(0, *A)
-            fetch(1, *A)
-            fetch(0, *B)
-            fetch(1, *B)
-            for c0, c1 in (A, B):
-                nc.vector.tensor_tensor(term[2][:, c0:c1], window[:].indirect(offsets(pos_sb[2], c0, c1)), gain2_sb[:, c0:c1], ALU.mult)
-            weigh(0, *A)
-            noise(2, *A)
-            weigh(1, *A)
-            noise(2, *B)
-            add(1, 0, *A)
-            weigh(0, *B)
-            add(2, 1, *A)
-            weigh(1, *B)
-            add(1, 0, *B)
-            limit(*A)
-            add(2, 1, *B0)
-            add(2, 1, *B1)
-            limit(*B0)
-            limit(*B1)
+            def limit(b):
+                nc.vector.scalar_tensor_tensor(result[:, block[b]], back[b][:], goal_sb[:], cap_sb[:, block[b]], ALU.mult, ALU.min)
+                put(block[b])
+
+            fetch(0, A)
+            fetch(0, B)
+            fetch(1, B)
+            fetch(2, block[3])
+            fused(2, A)
+            turn(2, True, False)
+            fused(1, A)
+            turn(1, False, False)
+            weigh(0, A)
+            turn(0, False, True)
+            for b in range(2):
+                nc.scalar.activation(ratio_t[:, b, :], turned[b][:], ACT.Identity, bias=noise_col[:, b : b + 1], scale=inv_col[:, b : b + 1])
+                nc.tensor.transpose(back[b][:], ratio_t[:, b, :], ident[:])
+            weigh(0, B)
+            fused(2, block[2])
+            weigh(1, B)
+            weigh(2, block[3])
+            for b in (2, 3):
+                nc.vector.scalar_tensor_tensor(acc[0][:, block[b]], term[0][:, block[b]], 0.1, term[1][:, block[b]], ALU.add, ALU.add)
+            for b in (2, 3):
+                nc.vector.tensor_tensor(acc[1][:, block[b]], acc[0][:, block[b]], term[2][:, block[b]], ALU.add)
+            limit(0)
+            for b in (2, 3):
+                nc.vector.scalar_tensor_tensor(acc[2][:, block[b]], acc[1][:, block[b]], goal_sb[:], inv_row[:, block[b - 2]], ALU.mult, ALU.mult)
+            limit(1)
+            for b in (2, 3):
+                nc.vector.tensor_tensor(result[:, block[b]], acc[2][:, block[b]], cap_sb[:, block[b]], ALU.min)
+                put(block[b])
 
         limited = keep.tile([P, S], F32, name="limited")
         final = keep.tile([P, S], F32, name="final")

@@ -35,7 +35,7 @@ def tile_picked_yfosch_two_p_kernel(
         scales = keep.tile([P, T], U8, name="scales", align_bytes=64)
         w_raw = keep.tile([P, PACK, M], F32, name="w_raw")
         gains = keep.tile([P, D, S], F32, name="gains")
-        owng_col = keep.tile([P, BLOCKS, 8], F32, name="owng_col")
+        owng_rows = keep.tile([P, P], F32, name="owng_rows")
         goal_sb = keep.tile([P, 1], F32, name="goal_sb")
         cap_sb = keep.tile([P, S], F32, name="cap_sb")
 
@@ -45,13 +45,12 @@ def tile_picked_yfosch_two_p_kernel(
             queue.dma_start(scales[32 * q : 32 * q + 32, :].bitcast(I32), rows.partition_broadcast(8))
         nc.sync.dma_start(w_raw[:], w1.rearrange("(p j) m -> p j m", j=PACK))
         nc.sync.dma_start(words[:], x_words[0].rearrange("p n t -> p (n t)").bitcast(I32))
-        with nc.allow_non_contiguous_dma(reason="one value a partition and block"):
-            nc.sync.dma_start(owng_col[:, :, 0], owng[0].rearrange("(b p) -> p b", p=P))
+        nc.sync.dma_start(owng_rows[:], owng[0 : P // BLOCKS].rearrange("r (b n) -> (r b) n", n=P))
         for d, pos in ((2, pos3), (0, pos1), (1, pos2)):
             nc.sync.dma_start(pos_sb[d][:], pos)
-        nc.sync.dma_start(goal_sb[:], goal)
         nc.sync.dma_start(gains[:], gain.rearrange("d p j -> p d j"))
         nc.sync.dma_start(cap_sb[:], cap)
+        nc.sync.dma_start(goal_sb[:], goal)
 
         ident = keep.tile([P, P], F32, name="ident")
         make_identity(nc, ident[:])
@@ -86,8 +85,10 @@ def tile_picked_yfosch_two_p_kernel(
 
         inv_col = keep.tile([P, BLOCKS], F32, name="inv_col", tag="table", align_bytes=64)
         noise_col = keep.tile([P, 2], F32, name="noise_col")
-        nc.vector.reciprocal(inv_col[:], owng_col[:, :, 0])
-        nc.vector.tensor_scalar(noise_col[:], inv_col[:, 0:2], 0.1, None, ALU.mult)
+        owng_t = psum.tile([P, P], F32, name="owng_t", tag="back0")
+        nc.tensor.transpose(owng_t[:], owng_rows[:], ident[:])
+        nc.vector.reciprocal(inv_col[:], owng_t[:, 0:BLOCKS])
+        nc.gpsimd.tensor_scalar(noise_col[:], inv_col[:, 0:2], 0.1, None, ALU.mult)
         inv_row = psum.tile([P, 2 * P], F32, name="inv_row")
         for b in range(2):
             nc.tensor.transpose(inv_row[:, b * P : (b + 1) * P], inv_col[:, 2 + b : 3 + b].to_broadcast([P, P]), ident[:])
@@ -101,7 +102,7 @@ def tile_picked_yfosch_two_p_kernel(
             term = [keep.tile([P, S], F32, name="term%d_%d" % (r, d)) for d in range(D)]
             acc = [keep.tile([P, S], F32, name="acc%d_%d" % (r, d)) for d in range(D)]
             turned = [psum.tile([P, P], F32, name="turned%d" % b) for b in range(2)]
-            back = [psum.tile([P, P], F32, name="back%d" % b) for b in range(2)]
+            back = [psum.tile([P, P], F32, name="back%d" % b, tag="back%d" % b) for b in range(2)]
             ratio_t = keep.tile([P, 2, P], F32, name="ratio_t%d" % r)
 
             def fetch(d, cols):

from contextlib import ExitStack

import concourse.mybir as mybir
from concourse.masks import make_identity

K, T, S, M, D = 512, 1024, 512, 128, 3
P = 128
PACK = 4
BLOCKS = S // P
FLOPS = 2 * K * M * S
BYTES = K * T + 16 * T + 4 * K * M + 4 * (D + 2) * S + 4 * M + 4 * 2 * P * S // 16 + 4 * M * S

F32 = mybir.dt.float32
BF16 = mybir.dt.bfloat16
I32 = mybir.dt.int32
U32 = mybir.dt.uint32
U16 = mybir.dt.uint16
U8 = mybir.dt.uint8
FP8X4 = mybir.dt.float8_e4m3fn_x4
ALU = mybir.AluOpType
ACT = mybir.ActivationFunctionType


def tile_picked_yfosch_two_p_kernel(
    tc, x_words, x_scales, w1, gain, owng, goal, cap, offs, pos1, pos2, pos3, out
):
    nc = tc.nc
    with ExitStack() as ctx:
        keep = ctx.enter_context(tc.tile_pool(name="keep", bufs=1))
        psum = ctx.enter_context(tc.psum_pool(name="psum", bufs=1))

        offs_sb = keep.tile([P, S // 16], U16, name="offs_sb")
        pos_sb = [keep.tile([P, S // 16], U16, name="pos_sb%d" % d) for d in range(D)]
        words = keep.tile([P, T], I32, name="words", tag="table", align_bytes=64)
        scales = keep.tile([P, T], U8, name="scales", align_bytes=64)
        w_raw = keep.tile([P, PACK, M], F32, name="w_raw")
        gains = keep.tile([P, D, S], F32, name="gains")
        owng_rows = keep.tile([P, P], F32, name="owng_rows")
        goal_sb = keep.tile([P, 1], F32, name="goal_sb")
        cap_sb = keep.tile([P, S], F32, name="cap_sb")

        nc.sync.dma_start(offs_sb[:], offs)
        for q, queue in enumerate((nc.sync, nc.scalar, nc.sync, nc.scalar)):
            rows = x_scales[0, 4 * q : 4 * q + 4, :].bitcast(I32)
            queue.dma_start(scales[32 * q : 32 * q + 32, :].bitcast(I32), rows.partition_broadcast(8))
        nc.sync.dma_start(w_raw[:], w1.rearrange("(p j) m -> p j m", j=PACK))
        nc.sync.dma_start(words[:], x_words[0].rearrange("p n t -> p (n t)").bitcast(I32))
        nc.sync.dma_start(owng_rows[:], owng[0 : P // BLOCKS].rearrange("r (b n) -> (r b) n", n=P))
        for d, pos in ((2, pos3), (0, pos1), (1, pos2)):
            nc.sync.dma_start(pos_sb[d][:], pos)
        nc.sync.dma_start(gains[:], gain.rearrange("d p j -> p d j"))
        nc.sync.dma_start(cap_sb[:], cap)
        nc.sync.dma_start(goal_sb[:], goal)

        ident = keep.tile([P, P], F32, name="ident")
        make_identity(nc, ident[:])

        w_bf = keep.tile([P, M, PACK], BF16, name="w_bf", tag="stage", align_bytes=64)
        nc.scalar.activation(w_bf[:], w_raw[:].rearrange("p j m -> p m j"), ACT.Copy)

        def offsets(lst, cols):
            return lst[:, cols.start // 16 : cols.stop // 16]

        picked_scales = keep.tile([P, S], U8, name="picked_scales", align_bytes=64)
        nc.vector.tensor_copy(picked_scales[:], scales[:].indirect(offs_sb[:]))
        w_codes = keep.tile([P, M], U32, name="w_codes", align_bytes=64)
        w_scales = keep.tile([P, M], U8, name="w_scales", align_bytes=64)
        nc.vector.quantize_mx(out=w_codes[:].bitcast(FP8X4), scales=w_scales[:], in_=w_bf[:].rearrange("p m j -> p (m j)"))

        picked_words = keep.tile([P, S], U32, name="picked_words", tag="stage", align_bytes=64)
        power = keep.tile([P, S], F32, name="power")
        for i, cols in enumerate((slice(0, 256), slice(256, 384), slice(384, 512))):
            nc.vector.tensor_copy(picked_words[:, cols], words[:].bitcast(U32).indirect(offsets(offs_sb, cols)))
            y = psum.tile([P, cols.stop - cols.start], F32, name="y%d" % i)
            nc.tensor.matmul_mx(
                out=y[:],
                lhsT=w_codes[:].bitcast(FP8X4),
                lhsT_scale=w_scales[:],
                rhs=picked_words[:, cols].bitcast(FP8X4),
                rhs_scale=picked_scales[:, cols],
                start=True,
                stop=True,
            )
            nc.scalar.activation(power[:, cols], y[:], ACT.Exp, scale=0.4)

        inv_col = keep.tile([P, BLOCKS], F32, name="inv_col", tag="table", align_bytes=64)
        noise_col = keep.tile([P, 2], F32, name="noise_col")
        owng_t = psum.tile([P, P], F32, name="owng_t", tag="back0")
        nc.tensor.transpose(owng_t[:], owng_rows[:], ident[:])
        nc.vector.reciprocal(inv_col[:], owng_t[:, 0:BLOCKS])
        nc.gpsimd.tensor_scalar(noise_col[:], inv_col[:, 0:2], 0.1, None, ALU.mult)
        inv_row = psum.tile([P, 2 * P], F32, name="inv_row")
        for b in range(2):
            nc.tensor.transpose(inv_row[:, b * P : (b + 1) * P], inv_col[:, 2 + b : 3 + b].to_broadcast([P, P]), ident[:])

        block = [slice(b * P, (b + 1) * P) for b in range(BLOCKS)]
        A = slice(0, 2 * P)
        B = slice(2 * P, S)

        def one_round(r, window, result, store):
            heard = [keep.tile([P, S], F32, name="heard%d_%d" % (r, d)) for d in range(D)]
            term = [keep.tile([P, S], F32, name="term%d_%d" % (r, d)) for d in range(D)]
            acc = [keep.tile([P, S], F32, name="acc%d_%d" % (r, d)) for d in range(D)]
            turned = [psum.tile([P, P], F32, name="turned%d" % b) for b in range(2)]
            back = [psum.tile([P, P], F32, name="back%d" % b, tag="back%d" % b) for b in range(2)]
            ratio_t = keep.tile([P, 2, P], F32, name="ratio_t%d" % r)

            def fetch(d, cols):
                nc.scalar.activation(heard[d][:, cols], window[:].indirect(offsets(pos_sb[d], cols)), ACT.Copy)

            def fused(d, cols):
                nc.vector.tensor_tensor(term[d][:, cols], window[:].indirect(offsets(pos_sb[d], cols)), gains[:, d, cols], ALU.mult)

            def weigh(d, cols):
                nc.vector.tensor_tensor(term[d][:, cols], heard[d][:, cols], gains[:, d, cols], ALU.mult)

            def turn(d, first, last):
                for b in range(2):
                    nc.tensor.matmul(turned[b][:], term[d][:, block[b]], ident[:], start=first, stop=last, is_transpose=True)

            def put(cols):
                if store:
                    nc.sync.dma_start(out[:, cols], result[:, cols])

            def limit(b):
                nc.vector.scalar_tensor_tensor(result[:, block[b]], back[b][:], goal_sb[:], cap_sb[:, block[b]], ALU.mult, ALU.min)
                put(block[b])

            fetch(0, A)
            fetch(0, B)
            fetch(1, B)
            fetch(2, block[3])
            fused(2, A)
            turn(2, True, False)
            fused(1, A)
            turn(1, False, False)
            weigh(0, A)
            turn(0, False, True)
            for b in range(2):
                nc.scalar.activation(ratio_t[:, b, :], turned[b][:], ACT.Identity, bias=noise_col[:, b : b + 1], scale=inv_col[:, b : b + 1])
                nc.tensor.transpose(back[b][:], ratio_t[:, b, :], ident[:])
            weigh(0, B)
            fused(2, block[2])
            weigh(1, B)
            weigh(2, block[3])
            for b in (2, 3):
                nc.vector.scalar_tensor_tensor(acc[0][:, block[b]], term[0][:, block[b]], 0.1, term[1][:, block[b]], ALU.add, ALU.add)
            for b in (2, 3):
                nc.vector.tensor_tensor(acc[1][:, block[b]], acc[0][:, block[b]], term[2][:, block[b]], ALU.add)
            limit(0)
            for b in (2, 3):
                nc.vector.scalar_tensor_tensor(acc[2][:, block[b]], acc[1][:, block[b]], goal_sb[:], inv_row[:, block[b - 2]], ALU.mult, ALU.mult)
            limit(1)
            for b in (2, 3):
                nc.vector.tensor_tensor(result[:, block[b]], acc[2][:, block[b]], cap_sb[:, block[b]], ALU.min)
                put(block[b])

        limited = keep.tile([P, S], F32, name="limited")
        final = keep.tile([P, S], F32, name="final")
        one_round(0, power, limited, False)
        one_round(1, limited, final, True)
